import numpy as np
import ml_dtypes


def mxq(x, axis, fmt="e4m3"):
    dtype, down = {"e4m3": (ml_dtypes.float8_e4m3fn, 7), "e5m2": (ml_dtypes.float8_e5m2, 14)}[fmt]
    v = np.moveaxis(np.asarray(x, np.float32).astype(ml_dtypes.bfloat16).astype(np.float64), axis, -1)
    blocks = v.reshape(v.shape[:-1] + (-1, 32))
    amax = np.abs(blocks).max(-1, keepdims=True)
    byte = np.maximum(np.where(amax > 0, np.frexp(amax)[1] - 1 + 127, 0) - down, 1)
    scale = np.exp2(byte - 127.0)
    codes = (blocks / scale).astype(np.float32).astype(dtype).astype(np.float64)
    return np.moveaxis((codes * scale).reshape(v.shape), -1, axis)


WIDE = False


def mx_kscale(k):
    if not WIDE:
        return np.ones(k)
    levels = np.array([10, -10, 5, -5, 0])
    if k % 512:
        return np.exp2(np.random.permutation(np.resize(levels, k // 32))).repeat(32)
    a = np.empty((k // 512, 16))
    for p in range(k // 512):
        a[p, :8] = np.random.permutation(np.resize(levels, 8))
        for g in range(8):
            far = levels[np.abs(levels - a[p, g]) >= 10]
            a[p, g + 8] = far[np.random.randint(len(far))]
    return np.exp2(a.ravel()).repeat(32)


def f64(x):
    return np.asarray(x).astype(np.float64)


def striped(idx):
    return np.tile(np.asarray(idx).reshape(-1, 16).T, (8, 1)).astype(np.uint16)


def unstriped(offs):
    return offs[:16].T.reshape(-1).astype(np.int64)


def striped8(idx):
    return np.asarray(idx).reshape(8, -1, 16).transpose(0, 2, 1).reshape(128, -1).astype(np.uint16)


def unstriped8(offs):
    return offs.reshape(8, 16, -1).transpose(0, 2, 1).reshape(8, -1).astype(np.int64)


def pick8(x, idx, run):
    r = np.arange(len(x))
    return x[r[:, None], idx[r % (8 * run) // run]]


E2M1 = np.array([0.0, 0.5, 1.0, 1.5, 2.0, 3.0, 4.0, 6.0, -0.0, -0.5, -1.0, -1.5, -2.0, -3.0, -4.0, -6.0])


def pack_weight(w, fmt):
    k, n = w.shape
    w = f64(np.asarray(w, np.float32).astype(ml_dtypes.bfloat16)).reshape(k // 32, 32, n)
    amax = np.abs(w).max(1)
    if fmt == "e4m3":
        byte = np.frexp(amax)[1] - 1 + 127 - 7
    else:
        mant, ex = np.frexp(amax / 6.0)
        byte = np.where(mant > 0.5, ex, ex - 1) + 127
    byte = np.clip(np.where(amax > 0, byte, 1), 1, 254)
    scaled = (w * np.exp2(127.0 - byte)[:, None, :]).reshape(k, n).astype(np.float32)
    by_word = np.ascontiguousarray(scaled.reshape(k // 512, 128, 4, n).transpose(0, 1, 3, 2))
    if fmt == "e4m3":
        words = by_word.astype(ml_dtypes.float8_e4m3fn).view(np.uint8)
    else:
        c = by_word.astype(ml_dtypes.float4_e2m1fn).view(np.uint8) & 0xF
        words = (c[..., 0::2] | (c[..., 1::2] << 4)).reshape(k // 512, 128, 2 * n)
    return np.ascontiguousarray(words), np.ascontiguousarray(byte.astype(np.uint8).reshape(k // 512, 16, n))


def unpack_weight(words, scales, fmt):
    g, _, n = scales.shape
    words = np.ascontiguousarray(words).reshape(g, 128, n, -1)
    if fmt == "e4m3":
        vals = words.view(ml_dtypes.float8_e4m3fn).astype(np.float64)
    else:
        nib = np.empty((g, 128, n, 4), np.uint8)
        nib[..., 0::2] = words & 0xF
        nib[..., 1::2] = words >> 4
        vals = E2M1[nib]
    vals = vals * np.repeat(np.exp2(scales.astype(np.float64) - 127.0), 8, axis=1)[..., None]
    return vals.transpose(0, 1, 3, 2).reshape(g * 512, n)


D, T, U, J, I = 512, 2048, 1024, 512, 512


def setup_inputs():
    n = np.random.standard_normal
    idx = np.stack([np.random.permutation(T)[:I] for _ in range(8)])
    idx2 = np.random.permutation(U)[:J]
    fd = mx_kscale(D)
    piecep = pack_weight(n((D, T)) / fd[:, None], "e4m3")
    return {
        "ent": (n((D, U)) * 1.2 / np.sqrt(D)).astype(np.float32),
        "fsc": (np.random.uniform(0.5, 1.5, (D, 1)) * fd[:, None]).astype(np.float32),
        "piece_words": piecep[0],
        "piece_scales": piecep[1],
        "steep": (np.random.uniform(0.5, 2.0, (J, 1))).astype(np.float32),
        "cwt": (np.random.uniform(0.5, 2.0, (1, I))).astype(np.float32),
        "bias": (0.3 * n((J, I))).astype(np.float32),
        "offs": striped8(idx),
        "offs2": striped(idx2),
    }


def reference(ent, fsc, piece_words, piece_scales, steep, cwt, bias, offs, offs2):
    idx = unstriped8(offs)
    idx2 = unstriped(offs2)
    pieceu = unpack_weight(piece_words, piece_scales, "e4m3")
    ex = f64(ent)[:, idx2] * f64(fsc)
    exq = mxq(ex, 0, "e4m3")
    pieceidxg = pick8(pieceu, idx, 64)
    a = exq.T @ pieceidxg
    y = np.tanh(a * f64(steep)) * f64(cwt) + f64(bias)
    return y

@@ -1,0 +1,159 @@
+from contextlib import ExitStack
+
+import concourse.mybir as mybir
+from concourse.masks import make_identity
+
+D, T, U, J, I = 512, 2048, 1024, 512, 512
+FLOPS = 2 * D * J * I
+
+F32 = mybir.dt.float32
+BF16 = mybir.dt.bfloat16
+I32 = mybir.dt.int32
+U32 = mybir.dt.uint32
+U16 = mybir.dt.uint16
+U8 = mybir.dt.uint8
+FP8X4 = mybir.dt.float8_e4m3fn_x4
+ACT = mybir.ActivationFunctionType
+ALU = mybir.AluOpType
+
+P = 128
+PACK = 4
+HALF = 256
+LIST_ROWS = 16
+
+
+def tile_attend_composedpairs_kernel(tc, ent, fsc, piece_words, piece_scales, steep, cwt, bias, offs, offs2, out):
+    nc = tc.nc
+    with ExitStack() as ctx:
+        keep = ctx.enter_context(tc.tile_pool(name="keep", bufs=1))
+        psum = ctx.enter_context(tc.psum_pool(name="psum", bufs=1))
+
+        piece_list = keep.tile([P, I // LIST_ROWS], U16, name="piece_list")
+        ent_list = keep.tile([P, J // LIST_ROWS], U16, name="ent_list")
+        scale_store = keep.tile([P, T], U8, name="scale_store")
+        nc.vector.memset(scale_store[:].bitcast(I32), 0)
+        warm_in = keep.tile([P, 1], F32, name="warm_in")
+        nc.vector.memset(warm_in[:], 0.0)
+        nc.scalar.dma_start(out=scale_store[0:P:8, :].bitcast(I32), in_=piece_scales[0].bitcast(I32))
+        nc.sync.dma_start(piece_list[:], offs)
+        nc.sync.dma_start(ent_list[:], offs2)
+
+        ent_rows = ent.rearrange("(p t) u -> t p u", t=PACK)
+        ent_plane = []
+        for t in range(PACK):
+            plane = keep.tile([P, U], F32, name="ent_plane%d" % t, tag="slot%d" % t)
+            nc.sync.dma_start(out=plane[:], in_=ent_rows[t])
+            ent_plane.append(plane)
+        word_store = keep.tile([P, T], I32, name="word_store")
+        nc.sync.dma_start(out=word_store[:], in_=piece_words[0].rearrange("p c r -> p (c r)").bitcast(I32))
+        fsc_cols = keep.tile([P, PACK], F32, name="fsc_cols")
+        nc.gpsimd.dma_start(out=fsc_cols[:], in_=fsc.rearrange("(p t) o -> p (t o)", t=PACK))
+        warm_out = keep.tile([P, 1], F32, name="warm_out")
+        nc.scalar.activation(out=warm_out[:], in_=warm_in[:], func=ACT.Tanh)
+
+        vec_rows = keep.tile([P, P], F32, name="vec_rows")
+        nc.vector.memset(vec_rows[:], 0.0)
+        nc.gpsimd.dma_start(out=vec_rows[0:4, :], in_=steep.rearrange("(m p) o -> m (p o)", p=P))
+        nc.gpsimd.dma_start(out=vec_rows[4:8, :], in_=cwt.rearrange("o (m p) -> (o m) p", p=P))
+        piece_plane = keep.tile([P, I], U8, name="piece_plane", align_bytes=64)
+        nc.vector.memset(piece_plane[:].bitcast(I32), 0)
+        ident = keep.tile([P, P], F32, name="ident")
+        make_identity(nc, ident[:])
+
+        scale_picked = keep.tile([P, I], U8, name="scale_picked")
+        nc.vector.tensor_copy(scale_picked[:], scale_store[:].indirect(piece_list[:]))
+        for r in range(4):
+            nc.scalar.dma_start(out=piece_plane[r:P:32, :].bitcast(I32), in_=scale_picked[8 * r : P : 32, :].bitcast(I32))
+
+        pairs = [keep.tile([P, 2, HALF, 2], BF16, name="pairs%d" % h) for h in range(2)]
+        woven = [keep.tile([P, HALF * PACK], BF16, name="woven%d" % h, align_bytes=64) for h in range(2)]
+        ex_codes = [keep.tile([P, HALF], U32, name="ex_codes%d" % h, align_bytes=64) for h in range(2)]
+        ex_plane = [keep.tile([P, HALF], U8, name="ex_plane%d" % h, align_bytes=64) for h in range(2)]
+        cols = HALF // LIST_ROWS
+
+        def scale(t, h, picked):
+            nc.scalar.activation(out=pairs[h][:, t // 2, :, t % 2], in_=picked, func=ACT.Copy, scale=fsc_cols[:, t : t + 1])
+
+        def gather_half(t, h):
+            picked = keep.tile([P, HALF], F32, name="picked%d_%d" % (t, h))
+            nc.vector.tensor_copy(picked[:], ent_plane[t][:].indirect(ent_list[:, h * cols : (h + 1) * cols]))
+            scale(t, h, picked[:])
+
+        def weave(h):
+            nc.scalar.copy(
+                out=woven[h][:].bitcast(U32).rearrange("p (j u) -> p j u", u=2),
+                in_=pairs[h][:].rearrange("p u j e -> p u (j e)").bitcast(U32).rearrange("p u j -> p j u"),
+            )
+
+        def quantize(h):
+            nc.vector.quantize_mx(out=ex_codes[h][:].bitcast(FP8X4), scales=ex_plane[h][:], in_=woven[h][:])
+
+        for t in range(2):
+            picked = keep.tile([P, J], F32, name="picked%d" % t)
+            nc.vector.tensor_copy(picked[:], ent_plane[t][:].indirect(ent_list[:]))
+            for h in range(2):
+                scale(t, h, picked[:, h * HALF : (h + 1) * HALF])
+
+        bias_rows = bias.rearrange("(g m p) i -> g p m i", m=2, p=P)
+        bias_sb = []
+        for g in range(2):
+            part = keep.tile([P, 2, I], F32, name="bias%d" % g, tag="slot%d" % g)
+            nc.sync.dma_start(out=part[:], in_=bias_rows[g])
+            bias_sb.append(part)
+
+        turned = psum.tile([P, P], F32, name="turned")
+        nc.tensor.transpose(turned[:], vec_rows[:], ident[:])
+        vec_cols = keep.tile([P, 8], F32, name="vec_cols")
+        nc.scalar.copy(out=vec_cols[:], in_=turned[:, 0:8])
+        cwt_all = psum.tile([P, I], F32, name="cwt_all")
+        for m in range(4):
+            nc.tensor.transpose(cwt_all[:, m * P : (m + 1) * P], vec_cols[:, 4 + m : 5 + m].to_broadcast([P, P]), ident[:])
+
+        for h in range(2):
+            gather_half(2, h)
+            gather_half(3, h)
+            weave(h)
+        quantize(0)
+
+        piece_codes = keep.tile([P, I], U32, name="piece_codes", align_bytes=64)
+        for h in range(2):
+            nc.vector.tensor_copy(
+                piece_codes[:, h * HALF : (h + 1) * HALF],
+                word_store[:].bitcast(U32).indirect(piece_list[:, h * cols : (h + 1) * cols]),
+            )
+        quantize(1)
+
+        units = [(0, 0, HALF), (1, 0, HALF), (0, HALF, I), (1, HALF, I), (2, 0, I), (3, 0, I)]
+        weighted = []
+
+        def score(n):
+            m, lo, hi = units[n]
+            acc = psum.tile([P, hi - lo], F32, name="acc%d" % n)
+            jc = slice((m % 2) * P, (m % 2 + 1) * P)
+            nc.tensor.matmul_mx(
+                out=acc[:],
+                lhsT=ex_codes[m // 2][:, jc].bitcast(FP8X4),
+                lhsT_scale=ex_plane[m // 2][:, jc],
+                rhs=piece_codes[:, lo:hi].bitcast(FP8X4),
+                rhs_scale=piece_plane[:, lo:hi],
+                start=True,
+                stop=True,
+            )
+            bent = keep.tile([P, hi - lo], F32, name="bent%d" % n)
+            nc.scalar.activation(out=bent[:], in_=acc[:], func=ACT.Tanh, scale=vec_cols[:, m : m + 1])
+            prod = keep.tile([P, hi - lo], F32, name="prod%d" % n)
+            nc.vector.tensor_tensor(prod[:], bent[:], cwt_all[:, lo:hi], ALU.mult)
+            weighted.append(prod)
+
+        def finish(n, a, b):
+            m, lo, hi = units[n]
+            res = keep.tile([P, b - a], F32, name="res%d_%d" % (n, a))
+            nc.vector.tensor_tensor(res[:], weighted[n][:, a:b], bias_sb[m // 2][:, m % 2, lo + a : lo + b], ALU.add)
+            nc.sync.dma_start(out=out[m * P : (m + 1) * P, lo + a : lo + b], in_=res[:])
+
+        score(0)
+        for n in range(1, len(units)):
+            score(n)
+            finish(n - 1, 0, units[n - 1][2] - units[n - 1][1])
+        finish(len(units) - 1, 0, HALF)
+        finish(len(units) - 1, HALF, I)

@@ -1,7 +1,6 @@
 from contextlib import ExitStack
 
 import concourse.mybir as mybir
-from concourse.masks import make_identity
 
 D, T, U, J, I = 512, 2048, 1024, 512, 512
 FLOPS = 2 * D * J * I
@@ -31,43 +30,50 @@ def tile_attend_composedpairs_kernel(tc, ent, fsc, piece_words, piece_scales, st
         piece_list = keep.tile([P, I // LIST_ROWS], U16, name="piece_list")
         ent_list = keep.tile([P, J // LIST_ROWS], U16, name="ent_list")
         scale_store = keep.tile([P, T], U8, name="scale_store")
-        nc.vector.memset(scale_store[:].bitcast(I32), 0)
-        warm_in = keep.tile([P, 1], F32, name="warm_in")
-        nc.vector.memset(warm_in[:], 0.0)
+        nc.gpsimd.memset(scale_store[:].bitcast(I32), 0)
         nc.scalar.dma_start(out=scale_store[0:P:8, :].bitcast(I32), in_=piece_scales[0].bitcast(I32))
         nc.sync.dma_start(piece_list[:], offs)
-        nc.sync.dma_start(ent_list[:], offs2)
 
         ent_rows = ent.rearrange("(p t) u -> t p u", t=PACK)
-        ent_plane = []
-        for t in range(PACK):
+        ent_plane = {}
+        for t in (0, 2, 1, 3):
             plane = keep.tile([P, U], F32, name="ent_plane%d" % t, tag="slot%d" % t)
             nc.sync.dma_start(out=plane[:], in_=ent_rows[t])
-            ent_plane.append(plane)
-        word_store = keep.tile([P, T], I32, name="word_store")
+            ent_plane[t] = plane[:]
+            if t == 0:
+                nc.sync.dma_start(ent_list[:], offs2)
+        word_store = keep.tile([P, T], I32, name="word_store", tag="store", align_bytes=64)
         nc.sync.dma_start(out=word_store[:], in_=piece_words[0].rearrange("p c r -> p (c r)").bitcast(I32))
         fsc_cols = keep.tile([P, PACK], F32, name="fsc_cols")
-        nc.gpsimd.dma_start(out=fsc_cols[:], in_=fsc.rearrange("(p t) o -> p (t o)", t=PACK))
-        warm_out = keep.tile([P, 1], F32, name="warm_out")
-        nc.scalar.activation(out=warm_out[:], in_=warm_in[:], func=ACT.Tanh)
+        nc.scalar.dma_start(out=fsc_cols[:], in_=fsc.rearrange("(p t) o -> p (t o)", t=PACK))
 
         vec_rows = keep.tile([P, P], F32, name="vec_rows")
         nc.vector.memset(vec_rows[:], 0.0)
-        nc.gpsimd.dma_start(out=vec_rows[0:4, :], in_=steep.rearrange("(m p) o -> m (p o)", p=P))
-        nc.gpsimd.dma_start(out=vec_rows[4:8, :], in_=cwt.rearrange("o (m p) -> (o m) p", p=P))
-        piece_plane = keep.tile([P, I], U8, name="piece_plane", align_bytes=64)
-        nc.vector.memset(piece_plane[:].bitcast(I32), 0)
+        nc.scalar.dma_start(out=vec_rows[0:4, :], in_=steep.rearrange("(m p) o -> m (p o)", p=P))
+        nc.scalar.dma_start(out=vec_rows[4:8, :], in_=cwt.rearrange("o (m p) -> (o m) p", p=P))
+        ones = keep.tile([P, P], F32, name="ones")
+        nc.vector.memset(ones[:], 1.0)
+        quad_first = keep.tile([P, 1], F32, name="quad_first")
+        for q in range(4):
+            nc.vector.memset(quad_first[32 * q : 32 * (q + 1), :], 32.0 * q)
+        ramp = keep.tile([P, P], F32, name="ramp", align_bytes=64)
+        nc.vector.tensor_tensor_scan(ramp[:], ones[:], ones[:], 0.0, ALU.mult, ALU.add)
+        in_quad = keep.tile([P, 32], F32, name="in_quad", align_bytes=64)
+        nc.vector.transpose(in_quad[:], ramp[:, 0:32])
         ident = keep.tile([P, P], F32, name="ident")
-        make_identity(nc, ident[:])
+        nc.vector.tensor_scalar(ident[:], ramp[:], in_quad[:, 0:1], quad_first[:], ALU.subtract, ALU.is_equal)
+        warm_out = keep.tile([P, 1], F32, name="warm_out")
+        nc.scalar.activation(out=warm_out[:], in_=ident[:, 0:1], func=ACT.Tanh)
 
         scale_picked = keep.tile([P, I], U8, name="scale_picked")
         nc.vector.tensor_copy(scale_picked[:], scale_store[:].indirect(piece_list[:]))
-        for r in range(4):
-            nc.scalar.dma_start(out=piece_plane[r:P:32, :].bitcast(I32), in_=scale_picked[8 * r : P : 32, :].bitcast(I32))
+        piece_plane = keep.tile([P, I], U8, name="piece_plane", align_bytes=64)
+        nc.vector.tensor_copy(piece_plane[:].bitcast(I32), scale_picked[:].bitcast(I32))
+        for r in range(1, 4):
+            nc.sync.dma_start(out=piece_plane[r:P:32, :].bitcast(I32), in_=scale_picked[8 * r : P : 32, :].bitcast(I32))
 
         pairs = [keep.tile([P, 2, HALF, 2], BF16, name="pairs%d" % h) for h in range(2)]
         woven = [keep.tile([P, HALF * PACK], BF16, name="woven%d" % h, align_bytes=64) for h in range(2)]
-        ex_codes = [keep.tile([P, HALF], U32, name="ex_codes%d" % h, align_bytes=64) for h in range(2)]
         ex_plane = [keep.tile([P, HALF], U8, name="ex_plane%d" % h, align_bytes=64) for h in range(2)]
         cols = HALF // LIST_ROWS
 
@@ -76,7 +82,7 @@ def tile_attend_composedpairs_kernel(tc, ent, fsc, piece_words, piece_scales, st
 
         def gather_half(t, h):
             picked = keep.tile([P, HALF], F32, name="picked%d_%d" % (t, h))
-            nc.vector.tensor_copy(picked[:], ent_plane[t][:].indirect(ent_list[:, h * cols : (h + 1) * cols]))
+            nc.vector.tensor_copy(picked[:], ent_plane[t].indirect(ent_list[:, h * cols : (h + 1) * cols]))
             scale(t, h, picked[:])
 
         def weave(h):
@@ -86,18 +92,18 @@ def tile_attend_composedpairs_kernel(tc, ent, fsc, piece_words, piece_scales, st
             )
 
         def quantize(h):
-            nc.vector.quantize_mx(out=ex_codes[h][:].bitcast(FP8X4), scales=ex_plane[h][:], in_=woven[h][:])
+            nc.vector.quantize_mx(out=ex_codes[:, h * HALF : (h + 1) * HALF].bitcast(FP8X4), scales=ex_plane[h][:], in_=woven[h][:])
 
-        for t in range(2):
+        for t in (0, 2):
             picked = keep.tile([P, J], F32, name="picked%d" % t)
-            nc.vector.tensor_copy(picked[:], ent_plane[t][:].indirect(ent_list[:]))
+            nc.vector.tensor_copy(picked[:], ent_plane[t].indirect(ent_list[:]))
             for h in range(2):
                 scale(t, h, picked[:, h * HALF : (h + 1) * HALF])
 
         bias_rows = bias.rearrange("(g m p) i -> g p m i", m=2, p=P)
         bias_sb = []
         for g in range(2):
-            part = keep.tile([P, 2, I], F32, name="bias%d" % g, tag="slot%d" % g)
+            part = keep.tile([P, 2, I], F32, name="bias%d" % g, tag="slot%d" % (2 * g))
             nc.sync.dma_start(out=part[:], in_=bias_rows[g])
             bias_sb.append(part)
 
@@ -110,20 +116,17 @@ def tile_attend_composedpairs_kernel(tc, ent, fsc, piece_words, piece_scales, st
             nc.tensor.transpose(cwt_all[:, m * P : (m + 1) * P], vec_cols[:, 4 + m : 5 + m].to_broadcast([P, P]), ident[:])
 
         for h in range(2):
-            gather_half(2, h)
+            gather_half(1, h)
             gather_half(3, h)
             weave(h)
-        quantize(0)
 
         piece_codes = keep.tile([P, I], U32, name="piece_codes", align_bytes=64)
-        for h in range(2):
-            nc.vector.tensor_copy(
-                piece_codes[:, h * HALF : (h + 1) * HALF],
-                word_store[:].bitcast(U32).indirect(piece_list[:, h * cols : (h + 1) * cols]),
-            )
+        nc.vector.tensor_copy(piece_codes[:], word_store[:].bitcast(U32).indirect(piece_list[:]))
+        ex_codes = keep.tile([P, J], U32, name="ex_codes", tag="store", align_bytes=64)
+        quantize(0)
         quantize(1)
 
-        units = [(0, 0, HALF), (1, 0, HALF), (0, HALF, I), (1, HALF, I), (2, 0, I), (3, 0, I)]
+        units = [(0, 0, HALF), (0, HALF, I), (1, 0, I), (2, 0, I), (3, 0, I)]
         weighted = []
 
         def score(n):
@@ -132,7 +135,7 @@ def tile_attend_composedpairs_kernel(tc, ent, fsc, piece_words, piece_scales, st
             jc = slice((m % 2) * P, (m % 2 + 1) * P)
             nc.tensor.matmul_mx(
                 out=acc[:],
-                lhsT=ex_codes[m // 2][:, jc].bitcast(FP8X4),
+                lhsT=ex_codes[:, m * P : (m + 1) * P].bitcast(FP8X4),
                 lhsT_scale=ex_plane[m // 2][:, jc],
                 rhs=piece_codes[:, lo:hi].bitcast(FP8X4),
                 rhs_scale=piece_plane[:, lo:hi],

@@ -19,6 +19,8 @@ P = 128
 PACK = 4
 HALF = 256
 LIST_ROWS = 16
+CHUNKS = ((0, 128), (128, 256), (256, 512))
+PLANE_ORDER = (0, 2, 1, 3)
 
 
 def tile_attend_composedpairs_kernel(tc, ent, fsc, piece_words, piece_scales, steep, cwt, bias, offs, offs2, out):
@@ -31,17 +33,15 @@ def tile_attend_composedpairs_kernel(tc, ent, fsc, piece_words, piece_scales, st
         ent_list = keep.tile([P, J // LIST_ROWS], U16, name="ent_list")
         scale_store = keep.tile([P, T], U8, name="scale_store")
         nc.gpsimd.memset(scale_store[:].bitcast(I32), 0)
-        nc.scalar.dma_start(out=scale_store[0:P:8, :].bitcast(I32), in_=piece_scales[0].bitcast(I32))
         nc.sync.dma_start(piece_list[:], offs)
+        nc.sync.dma_start(ent_list[:], offs2)
+        nc.sync.dma_start(out=scale_store[0:P:8, :].bitcast(I32), in_=piece_scales[0].bitcast(I32))
 
         ent_rows = ent.rearrange("(p t) u -> t p u", t=PACK)
         ent_plane = {}
-        for t in (0, 2, 1, 3):
-            plane = keep.tile([P, U], F32, name="ent_plane%d" % t, tag="slot%d" % t)
-            nc.sync.dma_start(out=plane[:], in_=ent_rows[t])
-            ent_plane[t] = plane[:]
-            if t == 0:
-                nc.sync.dma_start(ent_list[:], offs2)
+        for t in PLANE_ORDER:
+            ent_plane[t] = keep.tile([P, U], F32, name="ent_plane%d" % t, tag="slot%d" % t)
+            nc.sync.dma_start(out=ent_plane[t][:], in_=ent_rows[t])
         word_store = keep.tile([P, T], I32, name="word_store", tag="store", align_bytes=64)
         nc.sync.dma_start(out=word_store[:], in_=piece_words[0].rearrange("p c r -> p (c r)").bitcast(I32))
         fsc_cols = keep.tile([P, PACK], F32, name="fsc_cols")
@@ -68,44 +68,9 @@ def tile_attend_composedpairs_kernel(tc, ent, fsc, piece_words, piece_scales, st
         scale_picked = keep.tile([P, I], U8, name="scale_picked")
         nc.vector.tensor_copy(scale_picked[:], scale_store[:].indirect(piece_list[:]))
         piece_plane = keep.tile([P, I], U8, name="piece_plane", align_bytes=64)
-        nc.vector.tensor_copy(piece_plane[:].bitcast(I32), scale_picked[:].bitcast(I32))
-        for r in range(1, 4):
+        nc.gpsimd.memset(piece_plane[:].bitcast(I32), 0)
+        for r in range(4):
             nc.sync.dma_start(out=piece_plane[r:P:32, :].bitcast(I32), in_=scale_picked[8 * r : P : 32, :].bitcast(I32))
-
-        pairs = [keep.tile([P, 2, HALF, 2], BF16, name="pairs%d" % h) for h in range(2)]
-        woven = [keep.tile([P, HALF * PACK], BF16, name="woven%d" % h, align_bytes=64) for h in range(2)]
-        ex_plane = [keep.tile([P, HALF], U8, name="ex_plane%d" % h, align_bytes=64) for h in range(2)]
-        cols = HALF // LIST_ROWS
-
-        def scale(t, h, picked):
-            nc.scalar.activation(out=pairs[h][:, t // 2, :, t % 2], in_=picked, func=ACT.Copy, scale=fsc_cols[:, t : t + 1])
-
-        def gather_half(t, h):
-            picked = keep.tile([P, HALF], F32, name="picked%d_%d" % (t, h))
-            nc.vector.tensor_copy(picked[:], ent_plane[t].indirect(ent_list[:, h * cols : (h + 1) * cols]))
-            scale(t, h, picked[:])
-
-        def weave(h):
-            nc.scalar.copy(
-                out=woven[h][:].bitcast(U32).rearrange("p (j u) -> p j u", u=2),
-                in_=pairs[h][:].rearrange("p u j e -> p u (j e)").bitcast(U32).rearrange("p u j -> p j u"),
-            )
-
-        def quantize(h):
-            nc.vector.quantize_mx(out=ex_codes[:, h * HALF : (h + 1) * HALF].bitcast(FP8X4), scales=ex_plane[h][:], in_=woven[h][:])
-
-        for t in (0, 2):
-            picked = keep.tile([P, J], F32, name="picked%d" % t)
-            nc.vector.tensor_copy(picked[:], ent_plane[t].indirect(ent_list[:]))
-            for h in range(2):
-                scale(t, h, picked[:, h * HALF : (h + 1) * HALF])
-
-        bias_rows = bias.rearrange("(g m p) i -> g p m i", m=2, p=P)
-        bias_sb = []
-        for g in range(2):
-            part = keep.tile([P, 2, I], F32, name="bias%d" % g, tag="slot%d" % (2 * g))
-            nc.sync.dma_start(out=part[:], in_=bias_rows[g])
-            bias_sb.append(part)
 
         turned = psum.tile([P, P], F32, name="turned")
         nc.tensor.transpose(turned[:], vec_rows[:], ident[:])
@@ -115,28 +80,73 @@ def tile_attend_composedpairs_kernel(tc, ent, fsc, piece_words, piece_scales, st
         for m in range(4):
             nc.tensor.transpose(cwt_all[:, m * P : (m + 1) * P], vec_cols[:, 4 + m : 5 + m].to_broadcast([P, P]), ident[:])
 
-        for h in range(2):
-            gather_half(1, h)
-            gather_half(3, h)
-            weave(h)
+        pairs = [keep.tile([P, 2, hi - lo, 2], BF16, name="pairs%d" % lo) for lo, hi in CHUNKS]
+        woven = [keep.tile([P, (hi - lo) * PACK], BF16, name="woven%d" % lo, align_bytes=64) for lo, hi in CHUNKS]
+        ex_plane = [keep.tile([P, hi - lo], U8, name="ex_plane%d" % lo, align_bytes=64) for lo, hi in CHUNKS]
+        ex_codes = []
+
+        def gather(t, lo, hi):
+            picked = keep.tile([P, hi - lo], F32, name="picked%d_%d" % (t, lo))
+            nc.vector.tensor_copy(picked[:], ent_plane[t][:].indirect(ent_list[:, lo // LIST_ROWS : hi // LIST_ROWS]))
+            return picked
+
+        def scale(t, c, picked):
+            nc.scalar.activation(out=pairs[c][:, t // 2, :, t % 2], in_=picked, func=ACT.Copy, scale=fsc_cols[:, t : t + 1])
+
+        def weave(c):
+            copy, word = (nc.vector.tensor_copy, I32) if c == 0 else (nc.scalar.copy, U32)
+            copy(
+                out=woven[c][:].bitcast(word).rearrange("p (j u) -> p j u", u=2),
+                in_=pairs[c][:].rearrange("p u j e -> p u (j e)").bitcast(word).rearrange("p u j -> p j u"),
+            )
+
+        def quantize(c, codes):
+            ex_codes.append(codes)
+            nc.vector.quantize_mx(out=codes.bitcast(FP8X4), scales=ex_plane[c][:], in_=woven[c][:])
+
+        for t in PLANE_ORDER[:-1]:
+            for first in (0, HALF):
+                picked = gather(t, first, first + HALF)
+                for c, (lo, hi) in enumerate(CHUNKS):
+                    if first <= lo < first + HALF:
+                        scale(t, c, picked[:, lo - first : hi - first])
+
+        for c, (lo, hi) in enumerate(CHUNKS):
+            scale(PLANE_ORDER[-1], c, gather(PLANE_ORDER[-1], lo, hi)[:])
+        for c in range(len(CHUNKS)):
+            weave(c)
+        first_codes = keep.tile([P, P], U32, name="first_codes", align_bytes=64)
+        quantize(0, first_codes[:])
+
+        bias_rows = bias.rearrange("(g m p) i -> g p m i", m=2, p=P)
+        bias_sb = []
+        for g in range(2):
+            part = keep.tile([P, 2, I], F32, name="bias%d" % g, tag="slot%d" % PLANE_ORDER[2 + g])
+            nc.sync.dma_start(out=part[:], in_=bias_rows[g])
+            bias_sb.append(part)
 
         piece_codes = keep.tile([P, I], U32, name="piece_codes", align_bytes=64)
-        nc.vector.tensor_copy(piece_codes[:], word_store[:].bitcast(U32).indirect(piece_list[:]))
-        ex_codes = keep.tile([P, J], U32, name="ex_codes", tag="store", align_bytes=64)
-        quantize(0)
-        quantize(1)
+        for lo in (0, HALF):
+            nc.vector.tensor_copy(
+                piece_codes[:, lo : lo + HALF],
+                word_store[:].bitcast(U32).indirect(piece_list[:, lo // LIST_ROWS : (lo + HALF) // LIST_ROWS]),
+            )
+        later_codes = keep.tile([P, J - P], U32, name="later_codes", tag="store", align_bytes=64)
+        for c in range(1, len(CHUNKS)):
+            quantize(c, later_codes[:, CHUNKS[c][0] - P : CHUNKS[c][1] - P])
 
         units = [(0, 0, HALF), (0, HALF, I), (1, 0, I), (2, 0, I), (3, 0, I)]
         weighted = []
 
         def score(n):
             m, lo, hi = units[n]
+            c = [k for k, (a, b) in enumerate(CHUNKS) if a <= m * P < b][0]
+            jc = slice(m * P - CHUNKS[c][0], (m + 1) * P - CHUNKS[c][0])
             acc = psum.tile([P, hi - lo], F32, name="acc%d" % n)
-            jc = slice((m % 2) * P, (m % 2 + 1) * P)
             nc.tensor.matmul_mx(
                 out=acc[:],
-                lhsT=ex_codes[:, m * P : (m + 1) * P].bitcast(FP8X4),
-                lhsT_scale=ex_plane[m // 2][:, jc],
+                lhsT=ex_codes[c][:, jc].bitcast(FP8X4),
+                lhsT_scale=ex_plane[c][:, jc],
                 rhs=piece_codes[:, lo:hi].bitcast(FP8X4),
                 rhs_scale=piece_plane[:, lo:hi],
                 start=True,
@@ -148,15 +158,20 @@ def tile_attend_composedpairs_kernel(tc, ent, fsc, piece_words, piece_scales, st
             nc.vector.tensor_tensor(prod[:], bent[:], cwt_all[:, lo:hi], ALU.mult)
             weighted.append(prod)
 
-        def finish(n, a, b):
+        def finish(engine, n, a, b):
             m, lo, hi = units[n]
             res = keep.tile([P, b - a], F32, name="res%d_%d" % (n, a))
-            nc.vector.tensor_tensor(res[:], weighted[n][:, a:b], bias_sb[m // 2][:, m % 2, lo + a : lo + b], ALU.add)
+            engine.tensor_tensor(res[:], weighted[n][:, a:b], bias_sb[m // 2][:, m % 2, lo + a : lo + b], ALU.add)
             nc.sync.dma_start(out=out[m * P : (m + 1) * P, lo + a : lo + b], in_=res[:])
 
         score(0)
-        for n in range(1, len(units)):
-            score(n)
-            finish(n - 1, 0, units[n - 1][2] - units[n - 1][1])
-        finish(len(units) - 1, 0, HALF)
-        finish(len(units) - 1, HALF, I)
+        score(1)
+        finish(nc.vector, 0, 0, HALF)
+        finish(nc.vector, 1, 0, HALF)
+        score(2)
+        finish(nc.vector, 2, 0, I)
+        score(3)
+        score(4)
+        finish(nc.vector, 3, 0, I)
+        finish(nc.vector, 4, 0, HALF)
+        finish(nc.vector, 4, HALF, I)

@@ -17,10 +17,16 @@ ALU = mybir.AluOpType
 
 P = 128
 PACK = 4
-HALF = 256
+QUAD = 32
+BLOCK_ROWS = 8
 LIST_ROWS = 16
+ROW_TILES = J // P
+HALF = 256
+
 CHUNKS = ((0, 128), (128, 256), (256, 512))
+FIRST = 0
 PLANE_ORDER = (0, 2, 1, 3)
+PRODUCTS = ((0, 0, HALF), (0, HALF, I), (1, 0, I), (2, 0, I), (3, 0, I))
 
 
 def tile_attend_composedpairs_kernel(tc, ent, fsc, piece_words, piece_scales, steep, cwt, bias, offs, offs2, out):
@@ -35,12 +41,12 @@ def tile_attend_composedpairs_kernel(tc, ent, fsc, piece_words, piece_scales, st
         nc.gpsimd.memset(scale_store[:].bitcast(I32), 0)
         nc.sync.dma_start(piece_list[:], offs)
         nc.sync.dma_start(ent_list[:], offs2)
-        nc.sync.dma_start(out=scale_store[0:P:8, :].bitcast(I32), in_=piece_scales[0].bitcast(I32))
+        nc.sync.dma_start(out=scale_store[0:P:BLOCK_ROWS, :].bitcast(I32), in_=piece_scales[0].bitcast(I32))
 
         ent_rows = ent.rearrange("(p t) u -> t p u", t=PACK)
         ent_plane = {}
         for t in PLANE_ORDER:
-            ent_plane[t] = keep.tile([P, U], F32, name="ent_plane%d" % t, tag="slot%d" % t)
+            ent_plane[t] = keep.tile([P, U], F32, name="ent_plane%d" % t, tag="plane%d" % t)
             nc.sync.dma_start(out=ent_plane[t][:], in_=ent_rows[t])
         word_store = keep.tile([P, T], I32, name="word_store", tag="store", align_bytes=64)
         nc.sync.dma_start(out=word_store[:], in_=piece_words[0].rearrange("p c r -> p (c r)").bitcast(I32))
@@ -49,41 +55,44 @@ def tile_attend_composedpairs_kernel(tc, ent, fsc, piece_words, piece_scales, st
 
         vec_rows = keep.tile([P, P], F32, name="vec_rows")
         nc.vector.memset(vec_rows[:], 0.0)
-        nc.scalar.dma_start(out=vec_rows[0:4, :], in_=steep.rearrange("(m p) o -> m (p o)", p=P))
-        nc.scalar.dma_start(out=vec_rows[4:8, :], in_=cwt.rearrange("o (m p) -> (o m) p", p=P))
+        nc.scalar.dma_start(out=vec_rows[0:ROW_TILES, :], in_=steep.rearrange("(m p) o -> m (p o)", p=P))
+        nc.scalar.dma_start(out=vec_rows[ROW_TILES : 2 * ROW_TILES, :], in_=cwt.rearrange("o (m p) -> (o m) p", p=P))
+
         ones = keep.tile([P, P], F32, name="ones")
         nc.vector.memset(ones[:], 1.0)
         quad_first = keep.tile([P, 1], F32, name="quad_first")
-        for q in range(4):
-            nc.vector.memset(quad_first[32 * q : 32 * (q + 1), :], 32.0 * q)
+        for q in range(P // QUAD):
+            nc.vector.memset(quad_first[QUAD * q : QUAD * (q + 1), :], float(QUAD * q))
         ramp = keep.tile([P, P], F32, name="ramp", align_bytes=64)
         nc.vector.tensor_tensor_scan(ramp[:], ones[:], ones[:], 0.0, ALU.mult, ALU.add)
-        in_quad = keep.tile([P, 32], F32, name="in_quad", align_bytes=64)
-        nc.vector.transpose(in_quad[:], ramp[:, 0:32])
+        in_quad = keep.tile([P, QUAD], F32, name="in_quad", align_bytes=64)
+        nc.vector.transpose(in_quad[:], ramp[:, 0:QUAD])
         ident = keep.tile([P, P], F32, name="ident")
         nc.vector.tensor_scalar(ident[:], ramp[:], in_quad[:, 0:1], quad_first[:], ALU.subtract, ALU.is_equal)
-        warm_out = keep.tile([P, 1], F32, name="warm_out")
-        nc.scalar.activation(out=warm_out[:], in_=ident[:, 0:1], func=ACT.Tanh)
 
         scale_picked = keep.tile([P, I], U8, name="scale_picked")
         nc.vector.tensor_copy(scale_picked[:], scale_store[:].indirect(piece_list[:]))
         piece_plane = keep.tile([P, I], U8, name="piece_plane", align_bytes=64)
         nc.gpsimd.memset(piece_plane[:].bitcast(I32), 0)
-        for r in range(4):
-            nc.sync.dma_start(out=piece_plane[r:P:32, :].bitcast(I32), in_=scale_picked[8 * r : P : 32, :].bitcast(I32))
+        for r in range(QUAD // BLOCK_ROWS):
+            nc.sync.dma_start(
+                out=piece_plane[r:P:QUAD, :].bitcast(I32),
+                in_=scale_picked[BLOCK_ROWS * r : P : QUAD, :].bitcast(I32),
+            )
 
         turned = psum.tile([P, P], F32, name="turned")
         nc.tensor.transpose(turned[:], vec_rows[:], ident[:])
-        vec_cols = keep.tile([P, 8], F32, name="vec_cols")
-        nc.scalar.copy(out=vec_cols[:], in_=turned[:, 0:8])
+        vec_cols = keep.tile([P, 2 * ROW_TILES], F32, name="vec_cols")
+        nc.scalar.copy(out=vec_cols[:], in_=turned[:, 0 : 2 * ROW_TILES])
         cwt_all = psum.tile([P, I], F32, name="cwt_all")
-        for m in range(4):
-            nc.tensor.transpose(cwt_all[:, m * P : (m + 1) * P], vec_cols[:, 4 + m : 5 + m].to_broadcast([P, P]), ident[:])
+        for m in range(I // P):
+            spread = vec_cols[:, ROW_TILES + m : ROW_TILES + m + 1].to_broadcast([P, P])
+            nc.tensor.transpose(cwt_all[:, m * P : (m + 1) * P], spread, ident[:])
 
         pairs = [keep.tile([P, 2, hi - lo, 2], BF16, name="pairs%d" % lo) for lo, hi in CHUNKS]
         woven = [keep.tile([P, (hi - lo) * PACK], BF16, name="woven%d" % lo, align_bytes=64) for lo, hi in CHUNKS]
         ex_plane = [keep.tile([P, hi - lo], U8, name="ex_plane%d" % lo, align_bytes=64) for lo, hi in CHUNKS]
-        ex_codes = []
+        ex_codes = {}
 
         def gather(t, lo, hi):
             picked = keep.tile([P, hi - lo], F32, name="picked%d_%d" % (t, lo))
@@ -94,14 +103,14 @@ def tile_attend_composedpairs_kernel(tc, ent, fsc, piece_words, piece_scales, st
             nc.scalar.activation(out=pairs[c][:, t // 2, :, t % 2], in_=picked, func=ACT.Copy, scale=fsc_cols[:, t : t + 1])
 
         def weave(c):
-            copy, word = (nc.vector.tensor_copy, I32) if c == 0 else (nc.scalar.copy, U32)
+            copy, word = (nc.vector.tensor_copy, I32) if c == FIRST else (nc.scalar.copy, U32)
             copy(
                 out=woven[c][:].bitcast(word).rearrange("p (j u) -> p j u", u=2),
                 in_=pairs[c][:].rearrange("p u j e -> p u (j e)").bitcast(word).rearrange("p u j -> p j u"),
             )
 
         def quantize(c, codes):
-            ex_codes.append(codes)
+            ex_codes[c] = codes
             nc.vector.quantize_mx(out=codes.bitcast(FP8X4), scales=ex_plane[c][:], in_=woven[c][:])
 
         for t in PLANE_ORDER[:-1]:
@@ -116,12 +125,12 @@ def tile_attend_composedpairs_kernel(tc, ent, fsc, piece_words, piece_scales, st
         for c in range(len(CHUNKS)):
             weave(c)
         first_codes = keep.tile([P, P], U32, name="first_codes", align_bytes=64)
-        quantize(0, first_codes[:])
+        quantize(FIRST, first_codes[:])
 
         bias_rows = bias.rearrange("(g m p) i -> g p m i", m=2, p=P)
         bias_sb = []
         for g in range(2):
-            part = keep.tile([P, 2, I], F32, name="bias%d" % g, tag="slot%d" % PLANE_ORDER[2 + g])
+            part = keep.tile([P, 2, I], F32, name="bias%d" % g, tag="plane%d" % PLANE_ORDER[2 + g])
             nc.sync.dma_start(out=part[:], in_=bias_rows[g])
             bias_sb.append(part)
 
@@ -132,21 +141,20 @@ def tile_attend_composedpairs_kernel(tc, ent, fsc, piece_words, piece_scales, st
                 word_store[:].bitcast(U32).indirect(piece_list[:, lo // LIST_ROWS : (lo + HALF) // LIST_ROWS]),
             )
         later_codes = keep.tile([P, J - P], U32, name="later_codes", tag="store", align_bytes=64)
-        for c in range(1, len(CHUNKS)):
+        for c in range(FIRST + 1, len(CHUNKS)):
             quantize(c, later_codes[:, CHUNKS[c][0] - P : CHUNKS[c][1] - P])
 
-        units = [(0, 0, HALF), (0, HALF, I), (1, 0, I), (2, 0, I), (3, 0, I)]
-        weighted = []
+        weighted = [keep.tile([P, I], F32, name="weighted%d" % m) for m in range(ROW_TILES)]
 
         def score(n):
-            m, lo, hi = units[n]
+            m, lo, hi = PRODUCTS[n]
             c = [k for k, (a, b) in enumerate(CHUNKS) if a <= m * P < b][0]
-            jc = slice(m * P - CHUNKS[c][0], (m + 1) * P - CHUNKS[c][0])
+            rows = slice(m * P - CHUNKS[c][0], (m + 1) * P - CHUNKS[c][0])
             acc = psum.tile([P, hi - lo], F32, name="acc%d" % n)
             nc.tensor.matmul_mx(
                 out=acc[:],
-                lhsT=ex_codes[c][:, jc].bitcast(FP8X4),
-                lhsT_scale=ex_plane[c][:, jc],
+                lhsT=ex_codes[c][:, rows].bitcast(FP8X4),
+                lhsT_scale=ex_plane[c][:, rows],
                 rhs=piece_codes[:, lo:hi].bitcast(FP8X4),
                 rhs_scale=piece_plane[:, lo:hi],
                 start=True,
@@ -154,24 +162,21 @@ def tile_attend_composedpairs_kernel(tc, ent, fsc, piece_words, piece_scales, st
             )
             bent = keep.tile([P, hi - lo], F32, name="bent%d" % n)
             nc.scalar.activation(out=bent[:], in_=acc[:], func=ACT.Tanh, scale=vec_cols[:, m : m + 1])
-            prod = keep.tile([P, hi - lo], F32, name="prod%d" % n)
-            nc.vector.tensor_tensor(prod[:], bent[:], cwt_all[:, lo:hi], ALU.mult)
-            weighted.append(prod)
+            nc.vector.tensor_tensor(weighted[m][:, lo:hi], bent[:], cwt_all[:, lo:hi], ALU.mult)
 
-        def finish(engine, n, a, b):
-            m, lo, hi = units[n]
-            res = keep.tile([P, b - a], F32, name="res%d_%d" % (n, a))
-            engine.tensor_tensor(res[:], weighted[n][:, a:b], bias_sb[m // 2][:, m % 2, lo + a : lo + b], ALU.add)
-            nc.sync.dma_start(out=out[m * P : (m + 1) * P, lo + a : lo + b], in_=res[:])
+        def finish(m, lo, hi):
+            res = keep.tile([P, hi - lo], F32, name="res%d_%d" % (m, lo))
+            nc.vector.tensor_tensor(res[:], weighted[m][:, lo:hi], bias_sb[m // 2][:, m % 2, lo:hi], ALU.add)
+            nc.sync.dma_start(out=out[m * P : (m + 1) * P, lo:hi], in_=res[:])
 
         score(0)
         score(1)
-        finish(nc.vector, 0, 0, HALF)
-        finish(nc.vector, 1, 0, HALF)
+        finish(0, 0, HALF)
+        finish(0, HALF, I)
         score(2)
-        finish(nc.vector, 2, 0, I)
         score(3)
+        finish(1, 0, I)
         score(4)
-        finish(nc.vector, 3, 0, I)
-        finish(nc.vector, 4, 0, HALF)
-        finish(nc.vector, 4, HALF, I)
+        finish(2, 0, I)
+        finish(3, 0, HALF)
+        finish(3, HALF, I)

from contextlib import ExitStack

import concourse.mybir as mybir

D, T, U, J, I = 512, 2048, 1024, 512, 512
FLOPS = 2 * D * J * I

F32 = mybir.dt.float32
BF16 = mybir.dt.bfloat16
I32 = mybir.dt.int32
U32 = mybir.dt.uint32
U16 = mybir.dt.uint16
U8 = mybir.dt.uint8
FP8X4 = mybir.dt.float8_e4m3fn_x4
ACT = mybir.ActivationFunctionType
ALU = mybir.AluOpType

P = 128
PACK = 4
QUAD = 32
BLOCK_ROWS = 8
LIST_ROWS = 16
ROW_TILES = J // P
HALF = 256

CHUNKS = ((0, 128), (128, 256), (256, 512))
FIRST = 0
PLANE_ORDER = (0, 2, 1, 3)
PRODUCTS = ((0, 0, HALF), (0, HALF, I), (1, 0, I), (2, 0, I), (3, 0, I))


def tile_attend_composedpairs_kernel(tc, ent, fsc, piece_words, piece_scales, steep, cwt, bias, offs, offs2, out):
    nc = tc.nc
    with ExitStack() as ctx:
        keep = ctx.enter_context(tc.tile_pool(name="keep", bufs=1))
        psum = ctx.enter_context(tc.psum_pool(name="psum", bufs=1))

        piece_list = keep.tile([P, I // LIST_ROWS], U16, name="piece_list")
        ent_list = keep.tile([P, J // LIST_ROWS], U16, name="ent_list")
        scale_store = keep.tile([P, T], U8, name="scale_store")
        nc.gpsimd.memset(scale_store[:].bitcast(I32), 0)
        nc.sync.dma_start(piece_list[:], offs)
        nc.sync.dma_start(ent_list[:], offs2)
        nc.sync.dma_start(out=scale_store[0:P:BLOCK_ROWS, :].bitcast(I32), in_=piece_scales[0].bitcast(I32))

        ent_rows = ent.rearrange("(p t) u -> t p u", t=PACK)
        ent_plane = {}
        for t in PLANE_ORDER:
            ent_plane[t] = keep.tile([P, U], F32, name="ent_plane%d" % t, tag="plane%d" % t)
            nc.sync.dma_start(out=ent_plane[t][:], in_=ent_rows[t])
        word_store = keep.tile([P, T], I32, name="word_store", tag="store", align_bytes=64)
        nc.sync.dma_start(out=word_store[:], in_=piece_words[0].rearrange("p c r -> p (c r)").bitcast(I32))
        fsc_cols = keep.tile([P, PACK], F32, name="fsc_cols")
        nc.scalar.dma_start(out=fsc_cols[:], in_=fsc.rearrange("(p t) o -> p (t o)", t=PACK))

        vec_rows = keep.tile([P, P], F32, name="vec_rows")
        nc.vector.memset(vec_rows[:], 0.0)
        nc.scalar.dma_start(out=vec_rows[0:ROW_TILES, :], in_=steep.rearrange("(m p) o -> m (p o)", p=P))
        nc.scalar.dma_start(out=vec_rows[ROW_TILES : 2 * ROW_TILES, :], in_=cwt.rearrange("o (m p) -> (o m) p", p=P))

        ones = keep.tile([P, P], F32, name="ones")
        nc.vector.memset(ones[:], 1.0)
        quad_first = keep.tile([P, 1], F32, name="quad_first")
        for q in range(P // QUAD):
            nc.vector.memset(quad_first[QUAD * q : QUAD * (q + 1), :], float(QUAD * q))
        ramp = keep.tile([P, P], F32, name="ramp", align_bytes=64)
        nc.vector.tensor_tensor_scan(ramp[:], ones[:], ones[:], 0.0, ALU.mult, ALU.add)
        in_quad = keep.tile([P, QUAD], F32, name="in_quad", align_bytes=64)
        nc.vector.transpose(in_quad[:], ramp[:, 0:QUAD])
        ident = keep.tile([P, P], F32, name="ident")
        nc.vector.tensor_scalar(ident[:], ramp[:], in_quad[:, 0:1], quad_first[:], ALU.subtract, ALU.is_equal)

        scale_picked = keep.tile([P, I], U8, name="scale_picked")
        nc.vector.tensor_copy(scale_picked[:], scale_store[:].indirect(piece_list[:]))
        piece_plane = keep.tile([P, I], U8, name="piece_plane", align_bytes=64)
        nc.gpsimd.memset(piece_plane[:].bitcast(I32), 0)
        for r in range(QUAD // BLOCK_ROWS):
            nc.sync.dma_start(
                out=piece_plane[r:P:QUAD, :].bitcast(I32),
                in_=scale_picked[BLOCK_ROWS * r : P : QUAD, :].bitcast(I32),
            )

        turned = psum.tile([P, P], F32, name="turned")
        nc.tensor.transpose(turned[:], vec_rows[:], ident[:])
        vec_cols = keep.tile([P, 2 * ROW_TILES], F32, name="vec_cols")
        nc.scalar.copy(out=vec_cols[:], in_=turned[:, 0 : 2 * ROW_TILES])
        cwt_all = psum.tile([P, I], F32, name="cwt_all")
        for m in range(I // P):
            spread = vec_cols[:, ROW_TILES + m : ROW_TILES + m + 1].to_broadcast([P, P])
            nc.tensor.transpose(cwt_all[:, m * P : (m + 1) * P], spread, ident[:])

        pairs = [keep.tile([P, 2, hi - lo, 2], BF16, name="pairs%d" % lo) for lo, hi in CHUNKS]
        woven = [keep.tile([P, (hi - lo) * PACK], BF16, name="woven%d" % lo, align_bytes=64) for lo, hi in CHUNKS]
        ex_plane = [keep.tile([P, hi - lo], U8, name="ex_plane%d" % lo, align_bytes=64) for lo, hi in CHUNKS]
        ex_codes = {}

        def gather(t, lo, hi):
            picked = keep.tile([P, hi - lo], F32, name="picked%d_%d" % (t, lo))
            nc.vector.tensor_copy(picked[:], ent_plane[t][:].indirect(ent_list[:, lo // LIST_ROWS : hi // LIST_ROWS]))
            return picked

        def scale(t, c, picked):
            nc.scalar.activation(out=pairs[c][:, t // 2, :, t % 2], in_=picked, func=ACT.Copy, scale=fsc_cols[:, t : t + 1])

        def weave(c):
            copy, word = (nc.vector.tensor_copy, I32) if c == FIRST else (nc.scalar.copy, U32)
            copy(
                out=woven[c][:].bitcast(word).rearrange("p (j u) -> p j u", u=2),
                in_=pairs[c][:].rearrange("p u j e -> p u (j e)").bitcast(word).rearrange("p u j -> p j u"),
            )

        def quantize(c, codes):
            ex_codes[c] = codes
            nc.vector.quantize_mx(out=codes.bitcast(FP8X4), scales=ex_plane[c][:], in_=woven[c][:])

        for t in PLANE_ORDER[:-1]:
            for first in (0, HALF):
                picked = gather(t, first, first + HALF)
                for c, (lo, hi) in enumerate(CHUNKS):
                    if first <= lo < first + HALF:
                        scale(t, c, picked[:, lo - first : hi - first])

        for c, (lo, hi) in enumerate(CHUNKS):
            scale(PLANE_ORDER[-1], c, gather(PLANE_ORDER[-1], lo, hi)[:])
        for c in range(len(CHUNKS)):
            weave(c)
        first_codes = keep.tile([P, P], U32, name="first_codes", align_bytes=64)
        quantize(FIRST, first_codes[:])

        bias_rows = bias.rearrange("(g m p) i -> g p m i", m=2, p=P)
        bias_sb = []
        for g in range(2):
            part = keep.tile([P, 2, I], F32, name="bias%d" % g, tag="plane%d" % PLANE_ORDER[2 + g])
            nc.sync.dma_start(out=part[:], in_=bias_rows[g])
            bias_sb.append(part)

        piece_codes = keep.tile([P, I], U32, name="piece_codes", align_bytes=64)
        for lo in (0, HALF):
            nc.vector.tensor_copy(
                piece_codes[:, lo : lo + HALF],
                word_store[:].bitcast(U32).indirect(piece_list[:, lo // LIST_ROWS : (lo + HALF) // LIST_ROWS]),
            )
        later_codes = keep.tile([P, J - P], U32, name="later_codes", tag="store", align_bytes=64)
        for c in range(FIRST + 1, len(CHUNKS)):
            quantize(c, later_codes[:, CHUNKS[c][0] - P : CHUNKS[c][1] - P])

        weighted = [keep.tile([P, I], F32, name="weighted%d" % m) for m in range(ROW_TILES)]

        def score(n):
            m, lo, hi = PRODUCTS[n]
            c = [k for k, (a, b) in enumerate(CHUNKS) if a <= m * P < b][0]
            rows = slice(m * P - CHUNKS[c][0], (m + 1) * P - CHUNKS[c][0])
            acc = psum.tile([P, hi - lo], F32, name="acc%d" % n)
            nc.tensor.matmul_mx(
                out=acc[:],
                lhsT=ex_codes[c][:, rows].bitcast(FP8X4),
                lhsT_scale=ex_plane[c][:, rows],
                rhs=piece_codes[:, lo:hi].bitcast(FP8X4),
                rhs_scale=piece_plane[:, lo:hi],
                start=True,
                stop=True,
            )
            bent = keep.tile([P, hi - lo], F32, name="bent%d" % n)
            nc.scalar.activation(out=bent[:], in_=acc[:], func=ACT.Tanh, scale=vec_cols[:, m : m + 1])
            nc.vector.tensor_tensor(weighted[m][:, lo:hi], bent[:], cwt_all[:, lo:hi], ALU.mult)

        def finish(m, lo, hi):
            res = keep.tile([P, hi - lo], F32, name="res%d_%d" % (m, lo))
            nc.vector.tensor_tensor(res[:], weighted[m][:, lo:hi], bias_sb[m // 2][:, m % 2, lo:hi], ALU.add)
            nc.sync.dma_start(out=out[m * P : (m + 1) * P, lo:hi], in_=res[:])

        score(0)
        score(1)
        finish(0, 0, HALF)
        finish(0, HALF, I)
        score(2)
        score(3)
        finish(1, 0, I)
        score(4)
        finish(2, 0, I)
        finish(3, 0, HALF)
        finish(3, HALF, I)
